import numpy as np, ml_dtypes
CORES = [56,64,184,192,312,320,440,448]
N = 8
TK = 128
def setup_inputs(rng):
    return {"x": rng.standard_normal((N, 128, TK), dtype=np.float32).astype(ml_dtypes.bfloat16), "w1": (rng.standard_normal((N, 128, 128), dtype=np.float32) / 8).astype(ml_dtypes.bfloat16), "w2": (rng.standard_normal((N, 128, 128), dtype=np.float32) / 8).astype(ml_dtypes.bfloat16)}
def setup_inputs_big(rng):
    d = setup_inputs(rng)
    for k in ("x", "w1", "w2"): d[k] = (d[k].astype(np.float32) * 1024.0).astype(d[k].dtype)
    return d
def setup_inputs_small(rng):
    d = setup_inputs(rng)
    for k in ("x", "w1", "w2"): d[k] = (d[k].astype(np.float32) * (1 / 1024.0)).astype(d[k].dtype)
    return d
def setup_inputs_apart(rng):
    d = setup_inputs(rng)
    f = (10.0 ** rng.permutation(np.linspace(-1.5, 1.5, N))).astype(np.float32).reshape(N, 1, 1)
    for k in ("x", "w1", "w2"): d[k] = (d[k].astype(np.float32) * f).astype(d[k].dtype)
    return d
def reference(x, w1, w2):
    X, W1, W2 = x.astype(np.float64), w1.astype(np.float64), w2.astype(np.float64)
    y = np.zeros((N, 128, TK))
    for r in range(N):
        for j in range(N):
            y[r] += W2[j].T @ np.maximum(W1[j].T @ X[r], 0.0)
    return {"y": y.astype(ml_dtypes.bfloat16 if x.dtype != np.float64 else np.float64)}

@@ -1,0 +1,164 @@
+from concourse.bass import DstId, RemoteDMATransfer
+from concourse.mybir import AluOpType
+
+N = 8
+D = 128
+W = 2 * D
+NBANK = 4
+
+SCRATCH = {
+    "wd": ("dram", [D, W], "bfloat16"),
+    "wall": ("sbuf", [D, N * W], "bfloat16"),
+    "xs": ("sbuf", [D, D], "bfloat16"),
+    "hs": ("sbuf", [D, N * D], "bfloat16"),
+    "zero": ("sbuf", [D, D], "float32"),
+    "ys": ("sbuf", [D, D], "bfloat16"),
+    "py": ("psum", [D, 512], "float32"),
+}
+for _b in range(NBANK):
+    SCRATCH["ph%d" % _b] = ("psum", [D, 512], "float32")
+
+SEMAPHORES = (["ld", "ldx", "feed", "sent", "zs", "yd", "yc", "st"]
+              + ["arr%d" % j for j in range(N)] + ["m%d" % j for j in range(N)] + ["h%d" % j for j in range(N)])
+
+
+def _chip_cores(topo, c):
+    n = topo.CORES_PER_CHIP
+    return [k for k in range(max(0, c - n + 1), c + n) if topo.host(k) == topo.host(c) and topo.chip(k) == topo.chip(c)]
+
+
+def _peers(topo, ranks, c):
+    direct = [r for r in ranks if r != c and topo.may_write(c, r)]
+    s = [r for r in direct if topo.same_plane(c, r)][0]
+    cb = [r for r in direct if not topo.same_plane(c, r)][0]
+    dg = [r for r in ranks if r not in (c, s, cb) and topo.may_write(s, r)][0]
+    cross = [r for r in ranks if r not in (c, s, cb, dg)]
+    near = [r for r in cross if topo.rack(topo.host(r)) == topo.rack(topo.host(c))]
+    far = [r for r in cross if r not in near]
+    return s, cb, dg, near, far
+
+
+def _owners(topo, ranks, c, same_die):
+    near = _peers(topo, ranks, c)[3]
+    return [k for k in _chip_cores(topo, c)
+            if k != c and all(topo.may_write(k, r) for r in near) and (topo.die(k) == topo.die(c)) == same_die]
+
+
+def _relays(topo, ranks, c):
+    cb = _peers(topo, ranks, c)[1]
+    out = list(zip(_owners(topo, ranks, cb, True), _peers(topo, ranks, cb)[3]))
+    out += list(zip(_owners(topo, ranks, c, False), _peers(topo, ranks, c)[3]))
+    return out
+
+
+def _engines(topo, src, dsts):
+    m = topo.mask(src, dsts[0])
+    for d in dsts[1:]:
+        m &= topo.mask(src, d)
+    return m, bin(m).count("1")
+
+
+def _ids(topo, src, dsts):
+    out = []
+    for d in dsts:
+        rid, pid = topo.addr(d, src)
+        out.append(DstId(rid=rid, pnc=pid))
+    return out
+
+
+def rank_program(g, core, T, topo):
+    ranks = list(T.cores)
+    rank = T.rank_of(core)
+    sem = T.sem
+
+    def slot(j):
+        return T.wall[:, j * W:(j + 1) * W]
+
+    if rank is None:
+        for j, src in enumerate(ranks):
+            for relay, dst in _relays(topo, ranks, src):
+                if relay != core:
+                    continue
+                fed = _engines(topo, src, [k for k, _ in _relays(topo, ranks, src)])[1]
+                m, n = _engines(topo, core, [dst])
+                rid, pid = topo.addr(dst, core)
+                g.wait_ge(sem.feed, fed)
+                g.remote_dma(out_ap=slot(j), in_ap=T.wd[:, :], remote_sem=sem["arr%d" % j], local_sem=sem.sent,
+                             pid=pid, routing_id=rid, dma_engine_mask=m)
+                g.wait_ge(sem.sent, n)
+        return
+
+    s, cb, dg, near, far = _peers(topo, ranks, core)
+    idx = {c: j for j, c in enumerate(ranks)}
+
+    g.sync.dma_start(T.wd[:, 0:D], T.w1[:, :]).then_inc(sem.ld, 16)
+    g.scalar.dma_start(T.wd[:, D:W], T.w2[:, :]).then_inc(sem.ld, 16)
+    g.sync.dma_start(T.xs[:, :], T.x[:, :]).then_inc(sem.ldx, 16)
+    g.scalar.dma_start(T.wall[:, rank * W + D:(rank + 1) * W], T.w2[:, :]).then_inc(sem.ldx, 16)
+    g.sync.dma_start(T.wall[:, rank * W:rank * W + D], T.w1[:, :]).then_inc(sem.ldx, 16)
+
+    sent = 0
+    g.wait_ge(sem.ld, 32)
+    feeds = [k for k, _ in _relays(topo, ranks, core)]
+    m, n = _engines(topo, core, feeds)
+    g.remote_dma_fused([RemoteDMATransfer(dst_ids=_ids(topo, core, feeds), dma_engine_mask=m, remote_sem=sem.feed,
+                                          srcs=[T.wd[:, :]], dsts=[T.wd[:, :] for _ in feeds], alu_op=0)],
+                       local_sem=sem.sent)
+    sent += n
+    m, n = _engines(topo, core, [s, cb])
+    g.remote_dma_fused([RemoteDMATransfer(dst_ids=_ids(topo, core, [s, cb]), dma_engine_mask=m,
+                                          remote_sem=sem["arr%d" % rank],
+                                          srcs=[T.wd[:, :]], dsts=[slot(rank), slot(rank)], alu_op=0)],
+                       local_sem=sem.sent)
+    sent += n
+    def adds(a, b):
+        return _engines(topo, a, [b])[1]
+
+    arrives = {}
+    arrives[s] = _engines(topo, s, [core, _peers(topo, ranks, s)[1]])[1]
+    arrives[cb] = _engines(topo, cb, [_peers(topo, ranks, cb)[0], core])[1]
+    arrives[dg] = adds(cb, core)
+    for src in near + far:
+        relay = [k for k, d in _relays(topo, ranks, src) if d == core][0]
+        arrives[src] = adds(relay, core)
+
+    g.wait_ge(sem["arr%d" % idx[s]], arrives[s])
+    m, n = _engines(topo, core, [cb])
+    rid, pid = topo.addr(cb, core)
+    g.remote_dma(out_ap=slot(idx[s]), in_ap=slot(idx[s]), remote_sem=sem["arr%d" % idx[s]], local_sem=sem.sent,
+                 pid=pid, routing_id=rid, dma_engine_mask=m)
+    sent += n
+    g.wait_ge(sem.sent, sent)
+
+    order = [core, s, cb, dg] + far + near
+    t, v = g.tensor, g.vector
+
+    def second(i):
+        j = idx[order[i]]
+        t.wait_ge(sem["h%d" % i], 1)
+        t.matmul(T.py[:, 0:D], T.wall[:, j * W + D:(j + 1) * W], T.hs[:, i * D:(i + 1) * D],
+                 i == 0, i == N - 1).then_inc(sem.yd, 1)
+
+    t.wait_ge(sem.ldx, 48)
+    for i, src in enumerate(order):
+        j = idx[src]
+        if i > 0:
+            t.wait_ge(sem["arr%d" % j], arrives[src])
+        t.matmul(T["ph%d" % (i % NBANK)][:, 0:D], T.wall[:, j * W:j * W + D], T.xs[:, :],
+                 True, True).then_inc(sem["m%d" % i], 1)
+        if i > 0:
+            second(i - 1)
+    second(N - 1)
+
+    v.memset(T.zero[:, :], 0.0).then_inc(sem.zs, 1)
+    v.wait_ge(sem.zs, 1)
+    for i in range(N):
+        v.wait_ge(sem["m%d" % i], 1)
+        v.tensor_tensor(T.hs[:, i * D:(i + 1) * D], T["ph%d" % (i % NBANK)][:, 0:D], T.zero[:, :],
+                        AluOpType.max).then_inc(sem["h%d" % i], 1)
+    v.wait_ge(sem.yd, N)
+    v.tensor_copy(T.ys[:, :], T.py[:, 0:D]).then_inc(sem.yc, 1)
+
+    g.sync.wait_ge(sem.yc, 1)
+    g.sync.dma_start(T.y[:, :], T.ys[:, :]).then_inc(sem.st, 16)
+    g.sync.wait_ge(sem.st, 16)

@@ -5,6 +5,10 @@ N = 8
 D = 128
 W = 2 * D
 NBANK = 4
+OFF_STEP = 1
+ON_STEP = 1
+HELP_STEP = 2
+DIRECT_STEP = 1
 
 SCRATCH = {
     "wd": ("dram", [D, W], "bfloat16"),
@@ -38,24 +42,34 @@ def _peers(topo, ranks, c):
     return s, cb, dg, near, far
 
 
-def _owners(topo, ranks, c, same_die):
+def _pick(topo, ranks, c, owner, same_die):
     near = _peers(topo, ranks, c)[3]
     return [k for k in _chip_cores(topo, c)
-            if k != c and all(topo.may_write(k, r) for r in near) and (topo.die(k) == topo.die(c)) == same_die]
+            if k != c and all(topo.may_write(k, r) for r in near) == owner and (topo.die(k) == topo.die(c)) == same_die]
 
 
-def _relays(topo, ranks, c):
-    cb = _peers(topo, ranks, c)[1]
-    out = list(zip(_owners(topo, ranks, cb, True), _peers(topo, ranks, cb)[3]))
-    out += list(zip(_owners(topo, ranks, c, False), _peers(topo, ranks, c)[3]))
-    return out
+def _helpers(topo, ranks, c):
+    s, cb, dg, near, _ = _peers(topo, ranks, c)
+    off = list(zip(_pick(topo, ranks, cb, True, True), _peers(topo, ranks, cb)[3])) + [(_pick(topo, ranks, s, False, True)[0], dg)]
+    on = list(zip(_pick(topo, ranks, c, True, False), near)) + [(_pick(topo, ranks, c, False, False)[0], cb)]
+    return off, on
 
 
-def _engines(topo, src, dsts):
-    m = topo.mask(src, dsts[0])
-    for d in dsts[1:]:
-        m &= topo.mask(src, d)
-    return m, bin(m).count("1")
+def _count(m):
+    return bin(m).count("1")
+
+
+def _thin(m, step):
+    return sum(1 << e for e in [e for e in range(m.bit_length()) if (m >> e) & 1][::step])
+
+
+def _feed_masks(topo, ranks, c):
+    off, on = _helpers(topo, ranks, c)
+    m_off = topo.mask(c, off[0][0])
+    for k, _ in off:
+        m_off &= topo.mask(c, k)
+    m_on = topo.mask(c, on[0][0]) & ~m_off
+    return _thin(m_off, OFF_STEP), _thin(m_on, ON_STEP)
 
 
 def _ids(topo, src, dsts):
@@ -76,16 +90,16 @@ def rank_program(g, core, T, topo):
 
     if rank is None:
         for j, src in enumerate(ranks):
-            for relay, dst in _relays(topo, ranks, src):
-                if relay != core:
-                    continue
-                fed = _engines(topo, src, [k for k, _ in _relays(topo, ranks, src)])[1]
-                m, n = _engines(topo, core, [dst])
-                rid, pid = topo.addr(dst, core)
-                g.wait_ge(sem.feed, fed)
-                g.remote_dma(out_ap=slot(j), in_ap=T.wd[:, :], remote_sem=sem["arr%d" % j], local_sem=sem.sent,
-                             pid=pid, routing_id=rid, dma_engine_mask=m)
-                g.wait_ge(sem.sent, n)
+            for part, m_feed in zip(_helpers(topo, ranks, src), _feed_masks(topo, ranks, src)):
+                for helper, dst in part:
+                    if helper != core:
+                        continue
+                    m = _thin(topo.mask(core, dst), HELP_STEP)
+                    rid, pid = topo.addr(dst, core)
+                    g.wait_ge(sem.feed, _count(m_feed))
+                    g.remote_dma(out_ap=slot(j), in_ap=T.wd[:, :], remote_sem=sem["arr%d" % j], local_sem=sem.sent,
+                                 pid=pid, routing_id=rid, dma_engine_mask=m)
+                    g.wait_ge(sem.sent, _count(m))
         return
 
     s, cb, dg, near, far = _peers(topo, ranks, core)
@@ -99,38 +113,27 @@ def rank_program(g, core, T, topo):
 
     sent = 0
     g.wait_ge(sem.ld, 32)
-    feeds = [k for k, _ in _relays(topo, ranks, core)]
-    m, n = _engines(topo, core, feeds)
-    g.remote_dma_fused([RemoteDMATransfer(dst_ids=_ids(topo, core, feeds), dma_engine_mask=m, remote_sem=sem.feed,
-                                          srcs=[T.wd[:, :]], dsts=[T.wd[:, :] for _ in feeds], alu_op=0)],
-                       local_sem=sem.sent)
-    sent += n
-    m, n = _engines(topo, core, [s, cb])
-    g.remote_dma_fused([RemoteDMATransfer(dst_ids=_ids(topo, core, [s, cb]), dma_engine_mask=m,
-                                          remote_sem=sem["arr%d" % rank],
-                                          srcs=[T.wd[:, :]], dsts=[slot(rank), slot(rank)], alu_op=0)],
-                       local_sem=sem.sent)
-    sent += n
-    def adds(a, b):
-        return _engines(topo, a, [b])[1]
-
-    arrives = {}
-    arrives[s] = _engines(topo, s, [core, _peers(topo, ranks, s)[1]])[1]
-    arrives[cb] = _engines(topo, cb, [_peers(topo, ranks, cb)[0], core])[1]
-    arrives[dg] = adds(cb, core)
-    for src in near + far:
-        relay = [k for k, d in _relays(topo, ranks, src) if d == core][0]
-        arrives[src] = adds(relay, core)
-
-    g.wait_ge(sem["arr%d" % idx[s]], arrives[s])
-    m, n = _engines(topo, core, [cb])
-    rid, pid = topo.addr(cb, core)
-    g.remote_dma(out_ap=slot(idx[s]), in_ap=slot(idx[s]), remote_sem=sem["arr%d" % idx[s]], local_sem=sem.sent,
+    for part, m in zip(_helpers(topo, ranks, core), _feed_masks(topo, ranks, core)):
+        cores = [k for k, _ in part]
+        g.remote_dma_fused([RemoteDMATransfer(dst_ids=_ids(topo, core, cores), dma_engine_mask=m, remote_sem=sem.feed,
+                                              srcs=[T.wd[:, :]], dsts=[T.wd[:, :] for _ in cores], alu_op=0)],
+                           local_sem=sem.sent)
+        sent += _count(m)
+    m = _thin(topo.mask(core, s), DIRECT_STEP)
+    rid, pid = topo.addr(s, core)
+    g.remote_dma(out_ap=slot(rank), in_ap=T.wd[:, :], remote_sem=sem["arr%d" % rank], local_sem=sem.sent,
                  pid=pid, routing_id=rid, dma_engine_mask=m)
-    sent += n
+    sent += _count(m)
     g.wait_ge(sem.sent, sent)
 
-    order = [core, s, cb, dg] + far + near
+    arrives = {s: _count(_thin(topo.mask(s, core), DIRECT_STEP))}
+    for src in ranks:
+        for part in _helpers(topo, ranks, src):
+            for helper, dst in part:
+                if dst == core:
+                    arrives[src] = _count(_thin(topo.mask(helper, core), HELP_STEP))
+
+    order = [core, s] + near + far + [cb, dg]
     t, v = g.tensor, g.vector
 
     def second(i):

@@ -5,10 +5,6 @@ N = 8
 D = 128
 W = 2 * D
 NBANK = 4
-OFF_STEP = 1
-ON_STEP = 1
-HELP_STEP = 2
-DIRECT_STEP = 1
 
 SCRATCH = {
     "wd": ("dram", [D, W], "bfloat16"),
@@ -48,28 +44,34 @@ def _pick(topo, ranks, c, owner, same_die):
             if k != c and all(topo.may_write(k, r) for r in near) == owner and (topo.die(k) == topo.die(c)) == same_die]
 
 
-def _helpers(topo, ranks, c):
-    s, cb, dg, near, _ = _peers(topo, ranks, c)
-    off = list(zip(_pick(topo, ranks, cb, True, True), _peers(topo, ranks, cb)[3])) + [(_pick(topo, ranks, s, False, True)[0], dg)]
-    on = list(zip(_pick(topo, ranks, c, True, False), near)) + [(_pick(topo, ranks, c, False, False)[0], cb)]
-    return off, on
-
-
 def _count(m):
     return bin(m).count("1")
 
 
-def _thin(m, step):
-    return sum(1 << e for e in [e for e in range(m.bit_length()) if (m >> e) & 1][::step])
+def _thin(m):
+    return sum(1 << e for e in [e for e in range(m.bit_length()) if (m >> e) & 1][::2])
 
 
-def _feed_masks(topo, ranks, c):
-    off, on = _helpers(topo, ranks, c)
-    m_off = topo.mask(c, off[0][0])
-    for k, _ in off:
-        m_off &= topo.mask(c, k)
-    m_on = topo.mask(c, on[0][0]) & ~m_off
-    return _thin(m_off, OFF_STEP), _thin(m_on, ON_STEP)
+def _helpers(topo, ranks, c):
+    s, cb, dg, near, _ = _peers(topo, ranks, c)
+    beyond = _peers(topo, ranks, cb)[3]
+    if c > s:
+        near, beyond = near[::-1], beyond[::-1]
+    over = _pick(topo, ranks, cb, True, True)[0]
+    diag = _pick(topo, ranks, s, False, True)[0]
+    mine = _pick(topo, ranks, c, True, False)
+    spare = _pick(topo, ranks, c, False, False)[0]
+    m_off = topo.mask(c, over) & topo.mask(c, diag)
+    m_on = topo.mask(c, spare) & ~m_off
+    return [(over, beyond, m_off & ~_thin(m_off), 0), (diag, [dg], _thin(m_off), 0),
+            (mine[0], [near[0]], m_on, 1), (mine[1], [near[1]], m_on, 1), (spare, [cb], m_on, 1)]
+
+
+def _deliver_mask(topo, helper, dsts):
+    m = topo.mask(helper, dsts[0])
+    for d in dsts[1:]:
+        m &= topo.mask(helper, d)
+    return m if len(dsts) > 1 else _thin(m)
 
 
 def _ids(topo, src, dsts):
@@ -90,16 +92,16 @@ def rank_program(g, core, T, topo):
 
     if rank is None:
         for j, src in enumerate(ranks):
-            for part, m_feed in zip(_helpers(topo, ranks, src), _feed_masks(topo, ranks, src)):
-                for helper, dst in part:
-                    if helper != core:
-                        continue
-                    m = _thin(topo.mask(core, dst), HELP_STEP)
-                    rid, pid = topo.addr(dst, core)
-                    g.wait_ge(sem.feed, _count(m_feed))
-                    g.remote_dma(out_ap=slot(j), in_ap=T.wd[:, :], remote_sem=sem["arr%d" % j], local_sem=sem.sent,
-                                 pid=pid, routing_id=rid, dma_engine_mask=m)
-                    g.wait_ge(sem.sent, _count(m))
+            for helper, dsts, m_feed, _ in _helpers(topo, ranks, src):
+                if helper != core:
+                    continue
+                m = _deliver_mask(topo, core, dsts)
+                g.wait_ge(sem.feed, _count(m_feed))
+                g.remote_dma_fused([RemoteDMATransfer(dst_ids=_ids(topo, core, dsts), dma_engine_mask=m,
+                                                      remote_sem=sem["arr%d" % j],
+                                                      srcs=[T.wd[:, :]], dsts=[slot(j) for _ in dsts], alu_op=0)],
+                                   local_sem=sem.sent)
+                g.wait_ge(sem.sent, _count(m))
         return
 
     s, cb, dg, near, far = _peers(topo, ranks, core)
@@ -113,27 +115,36 @@ def rank_program(g, core, T, topo):
 
     sent = 0
     g.wait_ge(sem.ld, 32)
-    for part, m in zip(_helpers(topo, ranks, core), _feed_masks(topo, ranks, core)):
-        cores = [k for k, _ in part]
+    for call in (0, 1):
+        by_mask = {}
+        for helper, _, m, k in _helpers(topo, ranks, core):
+            if k == call:
+                by_mask.setdefault(m, []).append(helper)
         g.remote_dma_fused([RemoteDMATransfer(dst_ids=_ids(topo, core, cores), dma_engine_mask=m, remote_sem=sem.feed,
-                                              srcs=[T.wd[:, :]], dsts=[T.wd[:, :] for _ in cores], alu_op=0)],
-                           local_sem=sem.sent)
-        sent += _count(m)
-    m = _thin(topo.mask(core, s), DIRECT_STEP)
+                                              srcs=[T.wd[:, :]], dsts=[T.wd[:, :] for _ in cores], alu_op=0)
+                            for m, cores in by_mask.items()], local_sem=sem.sent)
+        sent += sum(_count(m) for m in by_mask)
+    m = topo.mask(core, s)
     rid, pid = topo.addr(s, core)
     g.remote_dma(out_ap=slot(rank), in_ap=T.wd[:, :], remote_sem=sem["arr%d" % rank], local_sem=sem.sent,
                  pid=pid, routing_id=rid, dma_engine_mask=m)
     sent += _count(m)
     g.wait_ge(sem.sent, sent)
 
-    arrives = {s: _count(_thin(topo.mask(s, core), DIRECT_STEP))}
+    arrives = {s: _count(topo.mask(s, core))}
+    turn = {}
     for src in ranks:
-        for part in _helpers(topo, ranks, src):
-            for helper, dst in part:
-                if dst == core:
-                    arrives[src] = _count(_thin(topo.mask(helper, core), HELP_STEP))
+        hs = _helpers(topo, ranks, src)
+        for helper, dsts, _, _ in hs:
+            if core in dsts:
+                arrives[src] = _count(_deliver_mask(topo, helper, dsts))
+        if core in hs[0][1]:
+            turn[src] = hs[0][1].index(core)
+        for n, h in enumerate(hs[2:4]):
+            if core in h[1]:
+                turn[src] = n
 
-    order = [core, s] + near + far + [cb, dg]
+    order = [core, s] + sorted(near + far, key=lambda c: (turn[c], c in far)) + [dg, cb]
     t, v = g.tensor, g.vector
 
     def second(i):

@@ -4,22 +4,25 @@ from concourse.mybir import AluOpType
 N = 8
 D = 128
 W = 2 * D
-NBANK = 4
+HT = D // 2
+NBANK = 6
+LAG = 2
 
 SCRATCH = {
     "wd": ("dram", [D, W], "bfloat16"),
     "wall": ("sbuf", [D, N * W], "bfloat16"),
     "xs": ("sbuf", [D, D], "bfloat16"),
     "hs": ("sbuf", [D, N * D], "bfloat16"),
-    "zero": ("sbuf", [D, D], "float32"),
+    "zero": ("sbuf", [D, HT], "float32"),
     "ys": ("sbuf", [D, D], "bfloat16"),
-    "py": ("psum", [D, 512], "float32"),
+    "py0": ("psum", [D, 512], "float32"),
+    "py1": ("psum", [D, 512], "float32"),
 }
 for _b in range(NBANK):
     SCRATCH["ph%d" % _b] = ("psum", [D, 512], "float32")
 
-SEMAPHORES = (["ld", "ldx", "feed", "sent", "zs", "yd", "yc", "st"]
-              + ["arr%d" % j for j in range(N)] + ["m%d" % j for j in range(N)] + ["h%d" % j for j in range(N)])
+SEMAPHORES = (["ld", "ldx", "feed", "sent", "zs", "yd0", "yd1", "yc", "st"] + ["arr%d" % j for j in range(N)]
+              + ["m%d_%d" % (j, k) for j in range(N) for k in (0, 1)] + ["h%d_%d" % (j, k) for j in range(N) for k in (0, 1)])
 
 
 def _chip_cores(topo, c):
@@ -63,8 +66,8 @@ def _helpers(topo, ranks, c):
     spare = _pick(topo, ranks, c, False, False)[0]
     m_off = topo.mask(c, over) & topo.mask(c, diag)
     m_on = topo.mask(c, spare) & ~m_off
-    return [(over, beyond, m_off & ~_thin(m_off), 0), (diag, [dg], _thin(m_off), 0),
-            (mine[0], [near[0]], m_on, 1), (mine[1], [near[1]], m_on, 1), (spare, [cb], m_on, 1)]
+    return [(over, beyond, m_off & ~_thin(m_off)), (diag, [dg], _thin(m_off)),
+            (mine[0], [near[0]], m_on), (mine[1], [near[1]], m_on), (spare, [cb], m_on)]
 
 
 def _deliver_mask(topo, helper, dsts):
@@ -92,7 +95,7 @@ def rank_program(g, core, T, topo):
 
     if rank is None:
         for j, src in enumerate(ranks):
-            for helper, dsts, m_feed, _ in _helpers(topo, ranks, src):
+            for helper, dsts, m_feed in _helpers(topo, ranks, src):
                 if helper != core:
                     continue
                 m = _deliver_mask(topo, core, dsts)
@@ -113,17 +116,14 @@ def rank_program(g, core, T, topo):
     g.scalar.dma_start(T.wall[:, rank * W + D:(rank + 1) * W], T.w2[:, :]).then_inc(sem.ldx, 16)
     g.sync.dma_start(T.wall[:, rank * W:rank * W + D], T.w1[:, :]).then_inc(sem.ldx, 16)
 
-    sent = 0
     g.wait_ge(sem.ld, 32)
-    for call in (0, 1):
-        by_mask = {}
-        for helper, _, m, k in _helpers(topo, ranks, core):
-            if k == call:
-                by_mask.setdefault(m, []).append(helper)
-        g.remote_dma_fused([RemoteDMATransfer(dst_ids=_ids(topo, core, cores), dma_engine_mask=m, remote_sem=sem.feed,
-                                              srcs=[T.wd[:, :]], dsts=[T.wd[:, :] for _ in cores], alu_op=0)
-                            for m, cores in by_mask.items()], local_sem=sem.sent)
-        sent += sum(_count(m) for m in by_mask)
+    by_mask = {}
+    for helper, _, m in _helpers(topo, ranks, core):
+        by_mask.setdefault(m, []).append(helper)
+    g.remote_dma_fused([RemoteDMATransfer(dst_ids=_ids(topo, core, cores), dma_engine_mask=m, remote_sem=sem.feed,
+                                          srcs=[T.wd[:, :]], dsts=[T.wd[:, :] for _ in cores], alu_op=0)
+                        for m, cores in by_mask.items()], local_sem=sem.sent)
+    sent = sum(_count(m) for m in by_mask)
     m = topo.mask(core, s)
     rid, pid = topo.addr(s, core)
     g.remote_dma(out_ap=slot(rank), in_ap=T.wd[:, :], remote_sem=sem["arr%d" % rank], local_sem=sem.sent,
@@ -135,7 +135,7 @@ def rank_program(g, core, T, topo):
     turn = {}
     for src in ranks:
         hs = _helpers(topo, ranks, src)
-        for helper, dsts, _, _ in hs:
+        for helper, dsts, _ in hs:
             if core in dsts:
                 arrives[src] = _count(_deliver_mask(topo, helper, dsts))
         if core in hs[0][1]:
@@ -147,32 +147,42 @@ def rank_program(g, core, T, topo):
     order = [core, s] + sorted(near + far, key=lambda c: (turn[c], c in far)) + [dg, cb]
     t, v = g.tensor, g.vector
 
+    def bank(i, k):
+        return T["ph%d" % ((2 * i + k) % NBANK)][:, 0:HT]
+
+    def half(i, k):
+        return T.hs[:, i * D + k * HT:i * D + (k + 1) * HT]
+
     def second(i):
         j = idx[order[i]]
-        t.wait_ge(sem["h%d" % i], 1)
-        t.matmul(T.py[:, 0:D], T.wall[:, j * W + D:(j + 1) * W], T.hs[:, i * D:(i + 1) * D],
-                 i == 0, i == N - 1).then_inc(sem.yd, 1)
+        for k in (0, 1):
+            t.wait_ge(sem["h%d_%d" % (i, k)], 1)
+            t.matmul(T["py%d" % k][:, 0:HT], T.wall[:, j * W + D:(j + 1) * W], half(i, k),
+                     i == 0, i == N - 1).then_inc(sem["yd%d" % k], 1)
 
     t.wait_ge(sem.ldx, 48)
     for i, src in enumerate(order):
         j = idx[src]
         if i > 0:
             t.wait_ge(sem["arr%d" % j], arrives[src])
-        t.matmul(T["ph%d" % (i % NBANK)][:, 0:D], T.wall[:, j * W:j * W + D], T.xs[:, :],
-                 True, True).then_inc(sem["m%d" % i], 1)
-        if i > 0:
-            second(i - 1)
-    second(N - 1)
+        for k in (0, 1):
+            t.matmul(bank(i, k), T.wall[:, j * W:j * W + D], T.xs[:, k * HT:(k + 1) * HT],
+                     True, True).then_inc(sem["m%d_%d" % (i, k)], 1)
+        if i >= LAG:
+            second(i - LAG)
+    for i in range(N - LAG, N):
+        second(i)
 
     v.memset(T.zero[:, :], 0.0).then_inc(sem.zs, 1)
     v.wait_ge(sem.zs, 1)
     for i in range(N):
-        v.wait_ge(sem["m%d" % i], 1)
-        v.tensor_tensor(T.hs[:, i * D:(i + 1) * D], T["ph%d" % (i % NBANK)][:, 0:D], T.zero[:, :],
-                        AluOpType.max).then_inc(sem["h%d" % i], 1)
-    v.wait_ge(sem.yd, N)
-    v.tensor_copy(T.ys[:, :], T.py[:, 0:D]).then_inc(sem.yc, 1)
+        for k in (0, 1):
+            v.wait_ge(sem["m%d_%d" % (i, k)], 1)
+            v.tensor_tensor(half(i, k), bank(i, k), T.zero[:, :], AluOpType.max).then_inc(sem["h%d_%d" % (i, k)], 1)
+    for k in (0, 1):
+        v.wait_ge(sem["yd%d" % k], N)
+        v.tensor_copy(T.ys[:, k * HT:(k + 1) * HT], T["py%d" % k][:, 0:HT]).then_inc(sem.yc, 1)
 
-    g.sync.wait_ge(sem.yc, 1)
+    g.sync.wait_ge(sem.yc, 2)
     g.sync.dma_start(T.y[:, :], T.ys[:, :]).then_inc(sem.st, 16)
     g.sync.wait_ge(sem.st, 16)

@@ -9,7 +9,7 @@ NBANK = 6
 LAG = 2
 
 SCRATCH = {
-    "wd": ("dram", [D, W], "bfloat16"),
+    "wd": ("dram", [2 * D, D], "bfloat16"),
     "wall": ("sbuf", [D, N * W], "bfloat16"),
     "xs": ("sbuf", [D, D], "bfloat16"),
     "hs": ("sbuf", [D, N * D], "bfloat16"),
@@ -21,7 +21,8 @@ SCRATCH = {
 for _b in range(NBANK):
     SCRATCH["ph%d" % _b] = ("psum", [D, 512], "float32")
 
-SEMAPHORES = (["ld", "ldx", "feed", "sent", "zs", "yd0", "yd1", "yc", "st"] + ["arr%d" % j for j in range(N)]
+SEMAPHORES = (["ld0", "ld1", "ldx", "feed0", "feed1", "sent", "zs", "yd0", "yd1", "yc", "st"]
+              + ["arr%d_%d" % (j, p) for j in range(N) for p in (0, 1)]
               + ["m%d_%d" % (j, k) for j in range(N) for k in (0, 1)] + ["h%d_%d" % (j, k) for j in range(N) for k in (0, 1)])
 
 
@@ -61,7 +62,7 @@ def _helpers(topo, ranks, c):
     if c > s:
         near, beyond = near[::-1], beyond[::-1]
     over = _pick(topo, ranks, cb, True, True)[0]
-    diag = _pick(topo, ranks, s, False, True)[0]
+    diag = _pick(topo, ranks, s, True, True)[1]
     mine = _pick(topo, ranks, c, True, False)
     spare = _pick(topo, ranks, c, False, False)[0]
     m_off = topo.mask(c, over) & topo.mask(c, diag)
@@ -74,7 +75,7 @@ def _deliver_mask(topo, helper, dsts):
     m = topo.mask(helper, dsts[0])
     for d in dsts[1:]:
         m &= topo.mask(helper, d)
-    return m if len(dsts) > 1 else _thin(m)
+    return m
 
 
 def _ids(topo, src, dsts):
@@ -90,8 +91,11 @@ def rank_program(g, core, T, topo):
     rank = T.rank_of(core)
     sem = T.sem
 
-    def slot(j):
-        return T.wall[:, j * W:(j + 1) * W]
+    def part(p):
+        return T.wd[p * D:(p + 1) * D, :]
+
+    def slot(j, p):
+        return T.wall[:, j * W + p * D:j * W + (p + 1) * D]
 
     if rank is None:
         for j, src in enumerate(ranks):
@@ -99,34 +103,39 @@ def rank_program(g, core, T, topo):
                 if helper != core:
                     continue
                 m = _deliver_mask(topo, core, dsts)
-                g.wait_ge(sem.feed, _count(m_feed))
-                g.remote_dma_fused([RemoteDMATransfer(dst_ids=_ids(topo, core, dsts), dma_engine_mask=m,
-                                                      remote_sem=sem["arr%d" % j],
-                                                      srcs=[T.wd[:, :]], dsts=[slot(j) for _ in dsts], alu_op=0)],
-                                   local_sem=sem.sent)
-                g.wait_ge(sem.sent, _count(m))
+                for p in (0, 1):
+                    g.wait_ge(sem["feed%d" % p], _count(m_feed))
+                    g.remote_dma_fused([RemoteDMATransfer(dst_ids=_ids(topo, core, dsts), dma_engine_mask=m,
+                                                          remote_sem=sem["arr%d_%d" % (j, p)],
+                                                          srcs=[part(p)], dsts=[slot(j, p) for _ in dsts], alu_op=0)],
+                                       local_sem=sem.sent)
+                g.wait_ge(sem.sent, 2 * _count(m))
         return
 
     s, cb, dg, near, far = _peers(topo, ranks, core)
     idx = {c: j for j, c in enumerate(ranks)}
 
-    g.sync.dma_start(T.wd[:, 0:D], T.w1[:, :]).then_inc(sem.ld, 16)
-    g.scalar.dma_start(T.wd[:, D:W], T.w2[:, :]).then_inc(sem.ld, 16)
+    g.sync.dma_start(part(0), T.w1[:, :]).then_inc(sem.ld0, 16)
+    g.scalar.dma_start(part(1), T.w2[:, :]).then_inc(sem.ld1, 16)
     g.sync.dma_start(T.xs[:, :], T.x[:, :]).then_inc(sem.ldx, 16)
     g.scalar.dma_start(T.wall[:, rank * W + D:(rank + 1) * W], T.w2[:, :]).then_inc(sem.ldx, 16)
     g.sync.dma_start(T.wall[:, rank * W:rank * W + D], T.w1[:, :]).then_inc(sem.ldx, 16)
 
-    g.wait_ge(sem.ld, 32)
     by_mask = {}
     for helper, _, m in _helpers(topo, ranks, core):
         by_mask.setdefault(m, []).append(helper)
-    g.remote_dma_fused([RemoteDMATransfer(dst_ids=_ids(topo, core, cores), dma_engine_mask=m, remote_sem=sem.feed,
-                                          srcs=[T.wd[:, :]], dsts=[T.wd[:, :] for _ in cores], alu_op=0)
-                        for m, cores in by_mask.items()], local_sem=sem.sent)
-    sent = sum(_count(m) for m in by_mask)
+    for p in (0, 1):
+        g.wait_ge(sem["ld%d" % p], 16)
+        g.remote_dma_fused([RemoteDMATransfer(dst_ids=_ids(topo, core, cores), dma_engine_mask=m,
+                                              remote_sem=sem["feed%d" % p],
+                                              srcs=[part(p)], dsts=[part(p) for _ in cores], alu_op=0)
+                            for m, cores in by_mask.items()], local_sem=sem.sent)
+    sent = 2 * sum(_count(m) for m in by_mask)
     m = topo.mask(core, s)
     rid, pid = topo.addr(s, core)
-    g.remote_dma(out_ap=slot(rank), in_ap=T.wd[:, :], remote_sem=sem["arr%d" % rank], local_sem=sem.sent,
+    own = T.wall[:, rank * W:(rank + 1) * W]
+    g.wait_ge(sem.ldx, 48)
+    g.remote_dma(out_ap=own, in_ap=own, remote_sem=sem["arr%d_0" % rank], local_sem=sem.sent,
                  pid=pid, routing_id=rid, dma_engine_mask=m)
     sent += _count(m)
     g.wait_ge(sem.sent, sent)
@@ -155,23 +164,26 @@ def rank_program(g, core, T, topo):
 
     def second(i):
         j = idx[order[i]]
+        if i > 1:
+            t.wait_ge(sem["arr%d_1" % j], arrives[order[i]])
         for k in (0, 1):
             t.wait_ge(sem["h%d_%d" % (i, k)], 1)
             t.matmul(T["py%d" % k][:, 0:HT], T.wall[:, j * W + D:(j + 1) * W], half(i, k),
                      i == 0, i == N - 1).then_inc(sem["yd%d" % k], 1)
 
     t.wait_ge(sem.ldx, 48)
+    nxt = [0]
     for i, src in enumerate(order):
         j = idx[src]
         if i > 0:
-            t.wait_ge(sem["arr%d" % j], arrives[src])
+            t.wait_ge(sem["arr%d_0" % j], arrives[src])
         for k in (0, 1):
             t.matmul(bank(i, k), T.wall[:, j * W:j * W + D], T.xs[:, k * HT:(k + 1) * HT],
                      True, True).then_inc(sem["m%d_%d" % (i, k)], 1)
-        if i >= LAG:
-            second(i - LAG)
-    for i in range(N - LAG, N):
-        second(i)
+        upto = i - LAG if i < N - 2 else (i - 1 if i == N - 2 else i)
+        while nxt[0] <= upto:
+            second(nxt[0])
+            nxt[0] += 1
 
     v.memset(T.zero[:, :], 0.0).then_inc(sem.zs, 1)
     v.wait_ge(sem.zs, 1)

from concourse.bass import DstId, RemoteDMATransfer
from concourse.mybir import AluOpType

N = 8
D = 128
W = 2 * D
HT = D // 2
NBANK = 6
LAG = 2

SCRATCH = {
    "wd": ("dram", [2 * D, D], "bfloat16"),
    "wall": ("sbuf", [D, N * W], "bfloat16"),
    "xs": ("sbuf", [D, D], "bfloat16"),
    "hs": ("sbuf", [D, N * D], "bfloat16"),
    "zero": ("sbuf", [D, HT], "float32"),
    "ys": ("sbuf", [D, D], "bfloat16"),
    "py0": ("psum", [D, 512], "float32"),
    "py1": ("psum", [D, 512], "float32"),
}
for _b in range(NBANK):
    SCRATCH["ph%d" % _b] = ("psum", [D, 512], "float32")

SEMAPHORES = (["ld0", "ld1", "ldx", "feed0", "feed1", "sent", "zs", "yd0", "yd1", "yc", "st"]
              + ["arr%d_%d" % (j, p) for j in range(N) for p in (0, 1)]
              + ["m%d_%d" % (j, k) for j in range(N) for k in (0, 1)] + ["h%d_%d" % (j, k) for j in range(N) for k in (0, 1)])


def _chip_cores(topo, c):
    n = topo.CORES_PER_CHIP
    return [k for k in range(max(0, c - n + 1), c + n) if topo.host(k) == topo.host(c) and topo.chip(k) == topo.chip(c)]


def _peers(topo, ranks, c):
    direct = [r for r in ranks if r != c and topo.may_write(c, r)]
    s = [r for r in direct if topo.same_plane(c, r)][0]
    cb = [r for r in direct if not topo.same_plane(c, r)][0]
    dg = [r for r in ranks if r not in (c, s, cb) and topo.may_write(s, r)][0]
    cross = [r for r in ranks if r not in (c, s, cb, dg)]
    near = [r for r in cross if topo.rack(topo.host(r)) == topo.rack(topo.host(c))]
    far = [r for r in cross if r not in near]
    return s, cb, dg, near, far


def _pick(topo, ranks, c, owner, same_die):
    near = _peers(topo, ranks, c)[3]
    return [k for k in _chip_cores(topo, c)
            if k != c and all(topo.may_write(k, r) for r in near) == owner and (topo.die(k) == topo.die(c)) == same_die]


def _count(m):
    return bin(m).count("1")


def _thin(m):
    return sum(1 << e for e in [e for e in range(m.bit_length()) if (m >> e) & 1][::2])


def _helpers(topo, ranks, c):
    s, cb, dg, near, _ = _peers(topo, ranks, c)
    beyond = _peers(topo, ranks, cb)[3]
    if c > s:
        near, beyond = near[::-1], beyond[::-1]
    over = _pick(topo, ranks, cb, True, True)[0]
    diag = _pick(topo, ranks, s, True, True)[1]
    mine = _pick(topo, ranks, c, True, False)
    spare = _pick(topo, ranks, c, False, False)[0]
    m_off = topo.mask(c, over) & topo.mask(c, diag)
    m_on = topo.mask(c, spare) & ~m_off
    return [(over, beyond, m_off & ~_thin(m_off)), (diag, [dg], _thin(m_off)),
            (mine[0], [near[0]], m_on), (mine[1], [near[1]], m_on), (spare, [cb], m_on)]


def _deliver_mask(topo, helper, dsts):
    m = topo.mask(helper, dsts[0])
    for d in dsts[1:]:
        m &= topo.mask(helper, d)
    return m


def _ids(topo, src, dsts):
    out = []
    for d in dsts:
        rid, pid = topo.addr(d, src)
        out.append(DstId(rid=rid, pnc=pid))
    return out


def rank_program(g, core, T, topo):
    ranks = list(T.cores)
    rank = T.rank_of(core)
    sem = T.sem

    def part(p):
        return T.wd[p * D:(p + 1) * D, :]

    def slot(j, p):
        return T.wall[:, j * W + p * D:j * W + (p + 1) * D]

    if rank is None:
        for j, src in enumerate(ranks):
            for helper, dsts, m_feed in _helpers(topo, ranks, src):
                if helper != core:
                    continue
                m = _deliver_mask(topo, core, dsts)
                for p in (0, 1):
                    g.wait_ge(sem["feed%d" % p], _count(m_feed))
                    g.remote_dma_fused([RemoteDMATransfer(dst_ids=_ids(topo, core, dsts), dma_engine_mask=m,
                                                          remote_sem=sem["arr%d_%d" % (j, p)],
                                                          srcs=[part(p)], dsts=[slot(j, p) for _ in dsts], alu_op=0)],
                                       local_sem=sem.sent)
                g.wait_ge(sem.sent, 2 * _count(m))
        return

    s, cb, dg, near, far = _peers(topo, ranks, core)
    idx = {c: j for j, c in enumerate(ranks)}

    g.sync.dma_start(part(0), T.w1[:, :]).then_inc(sem.ld0, 16)
    g.scalar.dma_start(part(1), T.w2[:, :]).then_inc(sem.ld1, 16)
    g.sync.dma_start(T.xs[:, :], T.x[:, :]).then_inc(sem.ldx, 16)
    g.scalar.dma_start(T.wall[:, rank * W + D:(rank + 1) * W], T.w2[:, :]).then_inc(sem.ldx, 16)
    g.sync.dma_start(T.wall[:, rank * W:rank * W + D], T.w1[:, :]).then_inc(sem.ldx, 16)

    by_mask = {}
    for helper, _, m in _helpers(topo, ranks, core):
        by_mask.setdefault(m, []).append(helper)
    for p in (0, 1):
        g.wait_ge(sem["ld%d" % p], 16)
        g.remote_dma_fused([RemoteDMATransfer(dst_ids=_ids(topo, core, cores), dma_engine_mask=m,
                                              remote_sem=sem["feed%d" % p],
                                              srcs=[part(p)], dsts=[part(p) for _ in cores], alu_op=0)
                            for m, cores in by_mask.items()], local_sem=sem.sent)
    sent = 2 * sum(_count(m) for m in by_mask)
    m = topo.mask(core, s)
    rid, pid = topo.addr(s, core)
    own = T.wall[:, rank * W:(rank + 1) * W]
    g.wait_ge(sem.ldx, 48)
    g.remote_dma(out_ap=own, in_ap=own, remote_sem=sem["arr%d_0" % rank], local_sem=sem.sent,
                 pid=pid, routing_id=rid, dma_engine_mask=m)
    sent += _count(m)
    g.wait_ge(sem.sent, sent)

    arrives = {s: _count(topo.mask(s, core))}
    turn = {}
    for src in ranks:
        hs = _helpers(topo, ranks, src)
        for helper, dsts, _ in hs:
            if core in dsts:
                arrives[src] = _count(_deliver_mask(topo, helper, dsts))
        if core in hs[0][1]:
            turn[src] = hs[0][1].index(core)
        for n, h in enumerate(hs[2:4]):
            if core in h[1]:
                turn[src] = n

    order = [core, s] + sorted(near + far, key=lambda c: (turn[c], c in far)) + [dg, cb]
    t, v = g.tensor, g.vector

    def bank(i, k):
        return T["ph%d" % ((2 * i + k) % NBANK)][:, 0:HT]

    def half(i, k):
        return T.hs[:, i * D + k * HT:i * D + (k + 1) * HT]

    def second(i):
        j = idx[order[i]]
        if i > 1:
            t.wait_ge(sem["arr%d_1" % j], arrives[order[i]])
        for k in (0, 1):
            t.wait_ge(sem["h%d_%d" % (i, k)], 1)
            t.matmul(T["py%d" % k][:, 0:HT], T.wall[:, j * W + D:(j + 1) * W], half(i, k),
                     i == 0, i == N - 1).then_inc(sem["yd%d" % k], 1)

    t.wait_ge(sem.ldx, 48)
    nxt = [0]
    for i, src in enumerate(order):
        j = idx[src]
        if i > 0:
            t.wait_ge(sem["arr%d_0" % j], arrives[src])
        for k in (0, 1):
            t.matmul(bank(i, k), T.wall[:, j * W:j * W + D], T.xs[:, k * HT:(k + 1) * HT],
                     True, True).then_inc(sem["m%d_%d" % (i, k)], 1)
        upto = i - LAG if i < N - 2 else (i - 1 if i == N - 2 else i)
        while nxt[0] <= upto:
            second(nxt[0])
            nxt[0] += 1

    v.memset(T.zero[:, :], 0.0).then_inc(sem.zs, 1)
    v.wait_ge(sem.zs, 1)
    for i in range(N):
        for k in (0, 1):
            v.wait_ge(sem["m%d_%d" % (i, k)], 1)
            v.tensor_tensor(half(i, k), bank(i, k), T.zero[:, :], AluOpType.max).then_inc(sem["h%d_%d" % (i, k)], 1)
    for k in (0, 1):
        v.wait_ge(sem["yd%d" % k], N)
        v.tensor_copy(T.ys[:, k * HT:(k + 1) * HT], T["py%d" % k][:, 0:HT]).then_inc(sem.yc, 1)

    g.sync.wait_ge(sem.yc, 2)
    g.sync.dma_start(T.y[:, :], T.ys[:, :]).then_inc(sem.st, 16)
    g.sync.wait_ge(sem.st, 16)
